import numpy as np, ml_dtypes
CORES = [19,147,275,403]
N = 4
import mx_ref
NC, WT = 256, 1
BF = ml_dtypes.bfloat16
def setup_inputs(rng):
    def f(*shape):
        return mx_ref.flush((rng.standard_normal(shape, dtype=np.float32) * np.exp2(rng.integers(-2, 3, shape[:-1] + (1,)))).astype(BF))
    return {"w": f(N, 128, WT * 512), "x": f(N, 128, 4 * NC)}
def setup_inputs_blocks(rng):
    d = setup_inputs(rng)
    for k in ("w", "x"): d[k] = mx_ref.spread(d[k], rng, 4)
    return d
def setup_inputs_wide(rng):
    d = setup_inputs(rng)
    for k in ("w", "x"): d[k] = mx_ref.flush((d[k].astype(np.float32) * np.exp2(rng.integers(-8, 9, (N, 1, 1))).astype(np.float32)).astype(BF))
    return d
def setup_inputs_zeros(rng):
    d = setup_inputs(rng); v = d["x"].reshape(N, 128, -1, 4).copy()
    v[np.broadcast_to((rng.random((N, 1, v.shape[2], 1)) < 0.33), v.shape)] = 0
    d["x"] = v.reshape(d["x"].shape)
    return d
def reference(w, x):
    QW = [mx_ref.quantize(w[b // WT][:, 512 * (b % WT):512 * (b % WT) + 512]) for b in range(N * WT)]
    y = np.zeros((N, 128, N * WT * NC), np.float32)
    for r in range(N):
        qx = mx_ref.quantize(x[r])
        for b in range(N * WT):
            y[r][:, NC * b:NC * b + NC] = mx_ref.matmul(QW[b], qx)
    return {"y": y}

@@ -1,0 +1,133 @@
+from concourse.mybir import dt, ActivationFunctionType
+
+N = 4
+WC = 128
+NC = 256
+HALF = NC // 2
+BANK = 512
+
+SCRATCH = {
+    "wb": ("sbuf", [128, 4 * WC], "bfloat16"),
+    "xb": ("sbuf", [128, 4 * NC], "bfloat16"),
+    "qw": ("sbuf", [128, N * WC], "float8_e4m3fn_x4"),
+    "sw": ("sbuf", [128, N * WC], "uint8"),
+    "qx": ("sbuf", [128, NC], "float8_e4m3fn_x4"),
+    "sx": ("sbuf", [128, NC], "uint8"),
+    "ps": ("psum", [128, 2 * N * BANK], "float32"),
+    "yb": ("sbuf", [128, N * NC], "float32"),
+}
+SEMAPHORES = (["lw", "lx", "qws", "qxs", "sent", "passed", "st"]
+              + ["sc%d" % b for b in range(N)]
+              + ["cd%d" % b for b in range(N)]
+              + ["mm%d" % j for j in range(2 * N)]
+              + ["cp%d" % b for b in range(N)])
+
+
+def rank_program(g, core, T, topo):
+    rank = T.rank_of(core)
+    if rank is None:
+        return
+    cores = list(T.cores)
+    ranks = range(len(cores))
+
+    def reach(a, b):
+        return a != b and topo.may_write(cores[a], cores[b])
+
+    def one_rack(a, b):
+        return topo.rack(topo.host(cores[a])) == topo.rack(topo.host(cores[b]))
+
+    def relay(o, d):
+        return [m for m in ranks if reach(o, m) and reach(m, d) and one_rack(m, d)][0]
+
+    def unreached(o):
+        return [d for d in ranks if d != o and not reach(o, d)]
+
+    def relays_of(o):
+        return [relay(o, d) for d in unreached(o)]
+
+    urgent = [d for d in ranks if reach(rank, d) and d in relays_of(rank)]
+    plain = [d for d in ranks if reach(rank, d) and d not in urgent]
+    onward = [(o, d) for o in ranks if o != rank for d in unreached(o) if d != rank and relay(o, d) == rank]
+    early = [o for o in ranks if reach(o, rank) and rank in relays_of(o)]
+    late = [o for o in ranks if reach(o, rank) and o not in early]
+    last = unreached(rank)
+
+    def cols(b):
+        return slice(WC * b, WC * b + WC)
+
+    def write(kind, o, d, local_sem):
+        rid, pid = topo.addr(cores[d], core)
+        mask = topo.mask(core, cores[d])
+        ap = T.sw[:, cols(o)] if kind == "sc" else T.qw[:, cols(o)].bitcast(dt.uint8)
+        g.remote_dma(out_ap=ap, in_ap=ap, remote_sem=T.sem[kind + "%d" % o], local_sem=local_sem,
+                     pid=pid, routing_id=rid, dma_engine_mask=mask)
+        return bin(mask).count("1")
+
+    def landed(o):
+        src = o if reach(o, rank) else relay(o, rank)
+        return bin(topo.mask(cores[src], core)).count("1")
+
+    g.sync.dma_start(T.wb[:], T.w[:]).then_inc(T.sem.lw, 16)
+    g.sync.dma_start(T.xb[:], T.x[:]).then_inc(T.sem.lx, 16)
+
+    g.vector.wait_ge(T.sem.lw, 16)
+    g.vector.quantize_mx(T.qw[:, cols(rank)], T.sw[:, cols(rank)], T.wb[:]).then_inc(T.sem.qws, 1)
+    g.vector.wait_ge(T.sem.lx, 16)
+    g.vector.quantize_mx(T.qx[:], T.sx[:], T.xb[:]).then_inc(T.sem.qxs, 1)
+
+    g.wait_ge(T.sem.qws, 1)
+    n_sent = 0
+    for d in urgent + plain:
+        n_sent += write("sc", rank, d, T.sem.sent)
+        n_sent += write("cd", rank, d, T.sem.sent)
+    n_passed = 0
+    for kind in ("sc", "cd"):
+        for o, d in onward:
+            g.wait_ge(T.sem[kind + "%d" % o], landed(o))
+            n_passed += write(kind, o, d, T.sem.passed)
+    g.wait_ge(T.sem.sent, n_sent)
+    g.wait_ge(T.sem.passed, n_passed)
+
+    order = [rank] + early + late + last
+    g.tensor.wait_ge(T.sem.qws, 1)
+    g.tensor.wait_ge(T.sem.qxs, 1)
+    for b in order:
+        if b != rank:
+            g.tensor.wait_ge(T.sem["sc%d" % b], landed(b))
+            g.tensor.wait_ge(T.sem["cd%d" % b], landed(b))
+        for h in range(2):
+            j = 2 * b + h
+            g.tensor.matmul_mx(T.ps[:, BANK * j:BANK * j + HALF], T.qw[:, cols(b)], T.sw[:, cols(b)],
+                               T.qx[:, HALF * h:HALF * h + HALF], T.sx[:, HALF * h:HALF * h + HALF],
+                               True, True).then_inc(T.sem["mm%d" % j], 1)
+
+    for b in order:
+        j = 2 * b
+        g.vector.wait_ge(T.sem["mm%d" % j], 1)
+        g.vector.tensor_copy(T.yb[:, NC * b:NC * b + HALF], T.ps[:, BANK * j:BANK * j + HALF]).then_inc(T.sem["cp%d" % b], 1)
+        j = 2 * b + 1
+        g.scalar.wait_ge(T.sem["mm%d" % j], 1)
+        g.scalar.activation(T.yb[:, NC * b + HALF:NC * b + NC], T.ps[:, BANK * j:BANK * j + HALF],
+                            ActivationFunctionType.Copy).then_inc(T.sem["cp%d" % b], 1)
+
+    n_st = [0]
+
+    def store(blocks):
+        for b in blocks:
+            g.sync.wait_ge(T.sem["cp%d" % b], 2)
+        bs = sorted(blocks)
+        runs = [[bs[0], bs[0]]]
+        for b in bs[1:]:
+            if b == runs[-1][1] + 1:
+                runs[-1][1] = b
+            else:
+                runs.append([b, b])
+        for lo, hi in runs:
+            g.sync.dma_start(T.y[:, NC * lo:NC * hi + NC], T.yb[:, NC * lo:NC * hi + NC]).then_inc(T.sem.st, 16)
+            n_st[0] += 16
+
+    store([rank] + late)
+    g.sync.wait_ge(T.sem.passed, n_passed)
+    store(early)
+    store(last)
+    g.sync.wait_ge(T.sem.st, n_st[0])

@@ -16,7 +16,7 @@ SCRATCH = {
     "ps": ("psum", [128, 2 * N * BANK], "float32"),
     "yb": ("sbuf", [128, N * NC], "float32"),
 }
-SEMAPHORES = (["lw", "lx", "qws", "qxs", "sent", "passed", "st"]
+SEMAPHORES = (["lw", "lx", "qws", "qxs", "sent", "passcd", "passsc", "st"]
               + ["sc%d" % b for b in range(N)]
               + ["cd%d" % b for b in range(N)]
               + ["mm%d" % j for j in range(2 * N)]
@@ -36,36 +36,39 @@ def rank_program(g, core, T, topo):
     def one_rack(a, b):
         return topo.rack(topo.host(cores[a])) == topo.rack(topo.host(cores[b]))
 
-    def relay(o, d):
-        return [m for m in ranks if reach(o, m) and reach(m, d) and one_rack(m, d)][0]
+    def relay(kind, o, d):
+        return [m for m in ranks if reach(o, m) and reach(m, d) and one_rack(m, d if kind == "cd" else o)][0]
 
     def unreached(o):
         return [d for d in ranks if d != o and not reach(o, d)]
 
-    def relays_of(o):
-        return [relay(o, d) for d in unreached(o)]
-
-    urgent = [d for d in ranks if reach(rank, d) and d in relays_of(rank)]
-    plain = [d for d in ranks if reach(rank, d) and d not in urgent]
-    onward = [(o, d) for o in ranks if o != rank for d in unreached(o) if d != rank and relay(o, d) == rank]
-    early = [o for o in ranks if reach(o, rank) and rank in relays_of(o)]
-    late = [o for o in ranks if reach(o, rank) and o not in early]
+    far = [d for d in ranks if reach(rank, d) and not one_rack(rank, d)]
+    near = [d for d in ranks if reach(rank, d) and one_rack(rank, d)]
     last = unreached(rank)
+
+    def onward(kind):
+        return [(o, d) for o in ranks if o != rank for d in unreached(o) if d != rank and relay(kind, o, d) == rank]
 
     def cols(b):
         return slice(WC * b, WC * b + WC)
 
+    def engines(o, src, dst):
+        mask = topo.mask(cores[src], cores[dst])
+        es = [e for e in range(mask.bit_length()) if (mask >> e) & 1]
+        if o == src:
+            es = es[1::2] if one_rack(src, dst) else es[0::2]
+        return es
+
     def write(kind, o, d, local_sem):
         rid, pid = topo.addr(cores[d], core)
-        mask = topo.mask(core, cores[d])
+        es = engines(o, rank, d)
         ap = T.sw[:, cols(o)] if kind == "sc" else T.qw[:, cols(o)].bitcast(dt.uint8)
         g.remote_dma(out_ap=ap, in_ap=ap, remote_sem=T.sem[kind + "%d" % o], local_sem=local_sem,
-                     pid=pid, routing_id=rid, dma_engine_mask=mask)
-        return bin(mask).count("1")
+                     pid=pid, routing_id=rid, dma_engine_mask=sum(1 << e for e in es))
+        return len(es)
 
-    def landed(o):
-        src = o if reach(o, rank) else relay(o, rank)
-        return bin(topo.mask(cores[src], core)).count("1")
+    def landed(kind, o):
+        return len(engines(o, o if reach(o, rank) else relay(kind, o, rank), rank))
 
     g.sync.dma_start(T.wb[:], T.w[:]).then_inc(T.sem.lw, 16)
     g.sync.dma_start(T.xb[:], T.x[:]).then_inc(T.sem.lx, 16)
@@ -77,24 +80,25 @@ def rank_program(g, core, T, topo):
 
     g.wait_ge(T.sem.qws, 1)
     n_sent = 0
-    for d in urgent + plain:
-        n_sent += write("sc", rank, d, T.sem.sent)
-        n_sent += write("cd", rank, d, T.sem.sent)
-    n_passed = 0
+    for kind, dsts in (("cd", far), ("sc", near), ("sc", far), ("cd", near)):
+        for d in dsts:
+            n_sent += write(kind, rank, d, T.sem.sent)
+    n_passed = {"cd": 0, "sc": 0}
     for kind in ("sc", "cd"):
-        for o, d in onward:
-            g.wait_ge(T.sem[kind + "%d" % o], landed(o))
-            n_passed += write(kind, o, d, T.sem.passed)
+        for o, d in onward(kind):
+            g.wait_ge(T.sem[kind + "%d" % o], landed(kind, o))
+            n_passed[kind] += write(kind, o, d, T.sem["pass" + kind])
     g.wait_ge(T.sem.sent, n_sent)
-    g.wait_ge(T.sem.passed, n_passed)
+    for kind in ("cd", "sc"):
+        g.wait_ge(T.sem["pass" + kind], n_passed[kind])
 
-    order = [rank] + early + late + last
+    order = [rank] + far + near + last
     g.tensor.wait_ge(T.sem.qws, 1)
     g.tensor.wait_ge(T.sem.qxs, 1)
     for b in order:
         if b != rank:
-            g.tensor.wait_ge(T.sem["sc%d" % b], landed(b))
-            g.tensor.wait_ge(T.sem["cd%d" % b], landed(b))
+            g.tensor.wait_ge(T.sem["sc%d" % b], landed("sc", b))
+            g.tensor.wait_ge(T.sem["cd%d" % b], landed("cd", b))
         for h in range(2):
             j = 2 * b + h
             g.tensor.matmul_mx(T.ps[:, BANK * j:BANK * j + HALF], T.qw[:, cols(b)], T.sw[:, cols(b)],
@@ -126,8 +130,8 @@ def rank_program(g, core, T, topo):
             g.sync.dma_start(T.y[:, NC * lo:NC * hi + NC], T.yb[:, NC * lo:NC * hi + NC]).then_inc(T.sem.st, 16)
             n_st[0] += 16
 
-    store([rank] + late)
-    g.sync.wait_ge(T.sem.passed, n_passed)
-    store(early)
+    g.sync.wait_ge(T.sem.passcd, n_passed["cd"])
+    store([rank] + far)
+    store(near)
     store(last)
     g.sync.wait_ge(T.sem.st, n_st[0])

from concourse.mybir import dt, ActivationFunctionType

N = 4
WC = 128
NC = 256
HALF = NC // 2
BANK = 512

SCRATCH = {
    "wb": ("sbuf", [128, 4 * WC], "bfloat16"),
    "xb": ("sbuf", [128, 4 * NC], "bfloat16"),
    "qw": ("sbuf", [128, N * WC], "float8_e4m3fn_x4"),
    "sw": ("sbuf", [128, N * WC], "uint8"),
    "qx": ("sbuf", [128, NC], "float8_e4m3fn_x4"),
    "sx": ("sbuf", [128, NC], "uint8"),
    "ps": ("psum", [128, 2 * N * BANK], "float32"),
    "yb": ("sbuf", [128, N * NC], "float32"),
}
SEMAPHORES = (["lw", "lx", "qws", "qxs", "sent", "passcd", "passsc", "st"]
              + ["sc%d" % b for b in range(N)]
              + ["cd%d" % b for b in range(N)]
              + ["mm%d" % j for j in range(2 * N)]
              + ["cp%d" % b for b in range(N)])


def rank_program(g, core, T, topo):
    rank = T.rank_of(core)
    if rank is None:
        return
    cores = list(T.cores)
    ranks = range(len(cores))

    def reach(a, b):
        return a != b and topo.may_write(cores[a], cores[b])

    def one_rack(a, b):
        return topo.rack(topo.host(cores[a])) == topo.rack(topo.host(cores[b]))

    def relay(kind, o, d):
        return [m for m in ranks if reach(o, m) and reach(m, d) and one_rack(m, d if kind == "cd" else o)][0]

    def unreached(o):
        return [d for d in ranks if d != o and not reach(o, d)]

    far = [d for d in ranks if reach(rank, d) and not one_rack(rank, d)]
    near = [d for d in ranks if reach(rank, d) and one_rack(rank, d)]
    last = unreached(rank)

    def onward(kind):
        return [(o, d) for o in ranks if o != rank for d in unreached(o) if d != rank and relay(kind, o, d) == rank]

    def cols(b):
        return slice(WC * b, WC * b + WC)

    def engines(o, src, dst):
        mask = topo.mask(cores[src], cores[dst])
        es = [e for e in range(mask.bit_length()) if (mask >> e) & 1]
        if o == src:
            es = es[1::2] if one_rack(src, dst) else es[0::2]
        return es

    def write(kind, o, d, local_sem):
        rid, pid = topo.addr(cores[d], core)
        es = engines(o, rank, d)
        ap = T.sw[:, cols(o)] if kind == "sc" else T.qw[:, cols(o)].bitcast(dt.uint8)
        g.remote_dma(out_ap=ap, in_ap=ap, remote_sem=T.sem[kind + "%d" % o], local_sem=local_sem,
                     pid=pid, routing_id=rid, dma_engine_mask=sum(1 << e for e in es))
        return len(es)

    def landed(kind, o):
        return len(engines(o, o if reach(o, rank) else relay(kind, o, rank), rank))

    g.sync.dma_start(T.wb[:], T.w[:]).then_inc(T.sem.lw, 16)
    g.sync.dma_start(T.xb[:], T.x[:]).then_inc(T.sem.lx, 16)

    g.vector.wait_ge(T.sem.lw, 16)
    g.vector.quantize_mx(T.qw[:, cols(rank)], T.sw[:, cols(rank)], T.wb[:]).then_inc(T.sem.qws, 1)
    g.vector.wait_ge(T.sem.lx, 16)
    g.vector.quantize_mx(T.qx[:], T.sx[:], T.xb[:]).then_inc(T.sem.qxs, 1)

    g.wait_ge(T.sem.qws, 1)
    n_sent = 0
    for kind, dsts in (("cd", far), ("sc", near), ("sc", far), ("cd", near)):
        for d in dsts:
            n_sent += write(kind, rank, d, T.sem.sent)
    n_passed = {"cd": 0, "sc": 0}
    for kind in ("sc", "cd"):
        for o, d in onward(kind):
            g.wait_ge(T.sem[kind + "%d" % o], landed(kind, o))
            n_passed[kind] += write(kind, o, d, T.sem["pass" + kind])
    g.wait_ge(T.sem.sent, n_sent)
    for kind in ("cd", "sc"):
        g.wait_ge(T.sem["pass" + kind], n_passed[kind])

    order = [rank] + far + near + last
    g.tensor.wait_ge(T.sem.qws, 1)
    g.tensor.wait_ge(T.sem.qxs, 1)
    for b in order:
        if b != rank:
            g.tensor.wait_ge(T.sem["sc%d" % b], landed("sc", b))
            g.tensor.wait_ge(T.sem["cd%d" % b], landed("cd", b))
        for h in range(2):
            j = 2 * b + h
            g.tensor.matmul_mx(T.ps[:, BANK * j:BANK * j + HALF], T.qw[:, cols(b)], T.sw[:, cols(b)],
                               T.qx[:, HALF * h:HALF * h + HALF], T.sx[:, HALF * h:HALF * h + HALF],
                               True, True).then_inc(T.sem["mm%d" % j], 1)

    for b in order:
        j = 2 * b
        g.vector.wait_ge(T.sem["mm%d" % j], 1)
        g.vector.tensor_copy(T.yb[:, NC * b:NC * b + HALF], T.ps[:, BANK * j:BANK * j + HALF]).then_inc(T.sem["cp%d" % b], 1)
        j = 2 * b + 1
        g.scalar.wait_ge(T.sem["mm%d" % j], 1)
        g.scalar.activation(T.yb[:, NC * b + HALF:NC * b + NC], T.ps[:, BANK * j:BANK * j + HALF],
                            ActivationFunctionType.Copy).then_inc(T.sem["cp%d" % b], 1)

    n_st = [0]

    def store(blocks):
        for b in blocks:
            g.sync.wait_ge(T.sem["cp%d" % b], 2)
        bs = sorted(blocks)
        runs = [[bs[0], bs[0]]]
        for b in bs[1:]:
            if b == runs[-1][1] + 1:
                runs[-1][1] = b
            else:
                runs.append([b, b])
        for lo, hi in runs:
            g.sync.dma_start(T.y[:, NC * lo:NC * hi + NC], T.yb[:, NC * lo:NC * hi + NC]).then_inc(T.sem.st, 16)
            n_st[0] += 16

    g.sync.wait_ge(T.sem.passcd, n_passed["cd"])
    store([rank] + far)
    store(near)
    store(last)
    g.sync.wait_ge(T.sem.st, n_st[0])
